import numpy as np, ml_dtypes
CORES = [4,20,36,44,92,100,108,116,3,19,35,43,91,99,107,115]
N = 16
KB, QP = 1, 64
ROOT = 7
def setup_inputs(rng):
    q = rng.standard_normal((N, 128, QP), dtype=np.float32) / 4; k = rng.standard_normal((N, 128, KB * 128), dtype=np.float32)
    a = 2 * np.pi * rng.random((N, QP)); s = 400 * rng.random((N, QP)) ** 1.5; q[:, 0, :] = s * np.cos(a); q[:, 1, :] = s * np.sin(a); q[:, 2, :] = 150 * rng.standard_normal((N, QP)); k[:, 2, :] = 1 + k[:, 2, :] / 50
    a = (2 * np.pi * rng.random() + np.pi / 2 * (rng.permutation(N).reshape(N, 1, 1) + 0.5) / N - 0.5 + (np.arange(KB).reshape(1, KB, 1) + rng.random((N, KB, 128))) / KB).reshape(N, KB * 128); k[:, 0, :] = np.cos(a); k[:, 1, :] = np.sin(a)
    for t in range(0, QP, 2):
        j, i = (t // 2) % N, rng.integers(KB * 128); q[ROOT, :2, t] = s[ROOT, t] * k[j, :2, i]; q[ROOT, 3:, t] += k[j, 3:, i] / 8
    return {"q": q.astype(ml_dtypes.bfloat16), "k": k.astype(ml_dtypes.bfloat16), "v": rng.standard_normal((N, 128, KB * 128), dtype=np.float32).astype(ml_dtypes.bfloat16)}
def setup_inputs_big(rng):
    d = setup_inputs(rng)
    for k in ("v",): d[k] = (d[k].astype(np.float32) * 1048576.0).astype(d[k].dtype)
    return d
def setup_inputs_small(rng):
    d = setup_inputs(rng)
    for k in ("v",): d[k] = (d[k].astype(np.float32) * (1 / 1048576.0)).astype(d[k].dtype)
    return d
def reference(q, k, v):
    Q, K, V = q.astype(np.float64), k.astype(np.float64), v.astype(np.float64)
    y = np.full((N, QP, 128), np.nan)
    for r in [ROOT]:
        js = list(range(N))
        S = np.concatenate([K[j].T @ Q[r] for j in js], axis=0)
        P = np.exp(S - S.max(axis=0)); P = P / P.sum(axis=0)
        y[r] = P.T @ np.concatenate([V[j][:, 128 * b:128 * b + 128] for j in js for b in range(KB)], axis=0)
    return {"y": y.astype(ml_dtypes.bfloat16)}

@@ -1,0 +1,331 @@
+from concourse.mybir import AluOpType, AxisListType, ActivationFunctionType
+
+NCORES = 128
+MAXG = 5
+MAXL = 3
+E_HOME = 16
+E_DIRECT = 8
+E_FEED = 8
+PASS_K = "rank"
+PASS_V = "rank"
+
+SCRATCH = {
+    "qs": ("sbuf", [128, 64], "bfloat16"),
+    "ko": ("sbuf", [128, 128], "bfloat16"),
+    "vo": ("sbuf", [128, 128], "bfloat16"),
+    "rk": ("sbuf", [128, 128], "bfloat16"),
+    "rv": ("sbuf", [128, 128], "bfloat16"),
+    "kall": ("sbuf", [128, 2048], "bfloat16"),
+    "vall": ("sbuf", [128, 2048], "bfloat16"),
+    "ones": ("sbuf", [128, 64], "bfloat16"),
+    "ident": ("sbuf", [128, 64], "bfloat16"),
+    "pt": ("sbuf", [128, 2048], "bfloat16"),
+    "p": ("sbuf", [128, 1024], "bfloat16"),
+    "accs": ("sbuf", [128, 128 * MAXG], "bfloat16"),
+    "nm": ("sbuf", [128, 8], "float32"),
+    "negm": ("sbuf", [128, 8], "float32"),
+    "l": ("sbuf", [128, 8], "float32"),
+    "w": ("sbuf", [128, 8], "float32"),
+    "lrun": ("sbuf", [128, 8], "float32"),
+    "lt": ("sbuf", [128, 8], "float32"),
+    "r": ("sbuf", [128, 8], "float32"),
+    "ysb": ("sbuf", [128, 128], "bfloat16"),
+    "s0": ("psum", [128, 512], "float32"),
+    "s1": ("psum", [128, 512], "float32"),
+    "s2": ("psum", [128, 512], "float32"),
+    "s3": ("psum", [128, 512], "float32"),
+    "s4": ("psum", [128, 512], "float32"),
+    "ptt0": ("psum", [128, 1024], "bfloat16"),
+    "ptt1": ("psum", [128, 1024], "bfloat16"),
+    "acc": ("psum", [128, 512], "float32"),
+}
+SEMAPHORES = (["ka%d" % i for i in range(MAXG)] + ["va%d" % i for i in range(MAXG)] +
+              ["kl%d" % i for i in range(MAXL)] + ["vl%d" % i for i in range(MAXL)] +
+              ["ldq", "ldk", "ldv", "rka", "rva", "sent", "i1", "i2",
+               "sS", "sR", "sM", "sE", "sW", "sT", "sP", "sA", "sO", "sL", "sC", "sY", "st",
+               "sSL", "sRL", "sEL", "sTL", "sPL", "sLL"])
+
+
+def _bits(mask, n):
+    out, k, b = 0, 0, 0
+    while k < n:
+        if (mask >> b) & 1:
+            out |= 1 << b
+            k += 1
+        b += 1
+    return out
+
+
+def _passer(T, topo, c, idx, root, direct, mode):
+    if mode == "rank":
+        return [d for d in direct if topo.chip(d) == topo.chip(c)][0]
+    free = [h for h in range(NCORES) if T.rank_of(h) is None and topo.may_write(h, root) and topo.may_write(c, h)]
+    if mode == "chip":
+        return [h for h in free if topo.chip(h) == topo.chip(c) and topo.die(h) == topo.die(c)][0]
+    cand = [h for h in free if topo.mates(topo.chip(h), topo.chip(root))]
+    cand.sort(key=lambda h: topo.die(h) != topo.die(c))
+    return cand[idx]
+
+
+def _plan(T, topo):
+    cores = list(T.cores)
+    root = cores[T.root]
+    rc = topo.chip(root)
+    home = [root] + [c for c in cores if topo.chip(c) == rc and c != root]
+    direct = [c for c in cores if topo.chip(c) != rc and topo.may_write(c, root)]
+    late = [c for c in cores if topo.chip(c) != rc and not topo.may_write(c, root)]
+
+    def way(c):
+        return (topo.die(c) != topo.die(root), not topo.same_plane(topo.chip(c), rc))
+
+    groups = [home]
+    for key in sorted(set(way(c) for c in direct)):
+        mem = [c for c in direct if way(c) == key]
+        for i in range(0, len(mem), 4):
+            groups.append(mem[i:i + 4])
+    groups.append(late)
+    pk, pv = {}, {}
+    for i, c in enumerate(late):
+        pk[c] = _passer(T, topo, c, i, root, direct, PASS_K)
+        pv[c] = _passer(T, topo, c, i, root, direct, PASS_V)
+    return root, groups, late, pk, pv
+
+
+def _write(g, T, topo, src, dst, out_ap, in_ap, rsem, n):
+    rid, pid, _ = topo.addr(dst)
+    g.remote_dma(out_ap, in_ap, remote_sem=rsem, local_sem=T.sem.sent, pid=pid, routing_id=rid,
+                 dma_engine_mask=_bits(topo.mask(src, dst), n))
+    return n
+
+
+def rank_program(g, core, T, topo):
+    root, groups, late, pk, pv = _plan(T, topo)
+    slot, grp = {}, {}
+    for gi, mem in enumerate(groups):
+        for c in mem:
+            grp[c] = gi
+            slot[c] = len(slot)
+    if core == root:
+        _root(g, core, T, topo, groups, slot)
+        return
+
+    sem = T.sem
+    sent = 0
+
+    def kslot(c):
+        return T.kall[:, slot[c] * 128:(slot[c] + 1) * 128]
+
+    def vslot(c):
+        return T.vall[:, slot[c] * 128:(slot[c] + 1) * 128]
+
+    if T.rank_of(core) is not None:
+        g.sync.dma_start(T.ko[:, :], T.k[:, :]).then_inc(sem.ldk, 16)
+        g.scalar.dma_start(T.vo[:, :], T.v[:, :]).then_inc(sem.ldv, 16)
+        if core in pk:
+            g.wait_ge(sem.ldk, 16)
+            sent += _write(g, T, topo, core, pk[core], T.rk[:, :], T.ko[:, :], sem.rka, E_FEED)
+            g.wait_ge(sem.ldv, 16)
+            sent += _write(g, T, topo, core, pv[core], T.rv[:, :], T.vo[:, :], sem.rva, E_FEED)
+        else:
+            n = E_HOME if topo.chip(core) == topo.chip(root) else E_DIRECT
+            g.wait_ge(sem.ldk, 16)
+            sent += _write(g, T, topo, core, root, kslot(core), T.ko[:, :], sem["ka%d" % grp[core]], n)
+            g.wait_ge(sem.ldv, 16)
+            sent += _write(g, T, topo, core, root, vslot(core), T.vo[:, :], sem["va%d" % grp[core]], n)
+    for b, c in enumerate(late):
+        if pk[c] == core:
+            g.wait_ge(sem.rka, E_FEED)
+            sent += _write(g, T, topo, core, root, kslot(c), T.rk[:, :], sem["kl%d" % b], E_DIRECT)
+        if pv[c] == core:
+            g.wait_ge(sem.rva, E_FEED)
+            sent += _write(g, T, topo, core, root, vslot(c), T.rv[:, :], sem["vl%d" % b], E_DIRECT)
+    if sent:
+        g.wait_ge(sem.sent, sent)
+
+
+def _root(g, core, T, topo, groups, slot):
+    sem = T.sem
+    G = len(groups)
+    GE = G - 1
+    Q = 64
+    pe, ve, ac = g.tensor, g.vector, g.scalar
+    Exp = ActivationFunctionType.Exp
+    first = [slot[mem[0]] for mem in groups]
+    nb = [len(mem) for mem in groups]
+    NL = nb[GE]
+    arr = []
+    for mem in groups[:GE]:
+        a = 0
+        for c in mem:
+            if c != core:
+                a += E_HOME if topo.chip(c) == topo.chip(core) else E_DIRECT
+        arr.append(a)
+
+    s0 = slot[core]
+    g.sync.dma_start(T.qs[:, :], T.q[:, :]).then_inc(sem.ldq, 16)
+    g.scalar.dma_start(T.kall[:, s0 * 128:(s0 + 1) * 128], T.k[:, :]).then_inc(sem.ldk, 16)
+    g.sync.dma_start(T.vall[:, s0 * 128:(s0 + 1) * 128], T.v[:, :]).then_inc(sem.ldv, 16)
+
+    ve.memset(T.ones[0:Q, :], 1.0).then_inc(sem.i1, 1)
+    g.wait_ge(sem.i1, 1)
+    g.affine_select(T.ident[0:Q, :], T.ones[0:Q, :], [[-1, Q]], AluOpType.is_equal, 0.0, 0, 1).then_inc(sem.i2, 1)
+    ident = T.ident[0:Q, 0:Q]
+
+    def sbank(i):
+        return T["s%d" % i][0:Q, 0:nb[i] * 128]
+
+    def col(t, i):
+        return t[0:Q, i:i + 1]
+
+    def kcols(s, n):
+        return T.kall[:, s * 128:(s + n) * 128]
+
+    def vcols(s):
+        return T.vall[:, s * 128:(s + 1) * 128]
+
+    def ptcols(s, n):
+        return T.pt[0:Q, s * 128:(s + n) * 128]
+
+    def pcols(s, n):
+        return T.p[:, s * Q:(s + n) * Q]
+
+    def accs(i):
+        return T.accs[0:Q, i * 128:(i + 1) * 128]
+
+    acc = T.acc[0:Q, 0:128]
+    tcount = [0]
+    lbank = [T["s%d" % i][0:Q, 0:128] for i in ([GE] + list(range(NL - 1)))]
+    lptt = [T.ptt0[:, 0:Q], T.ptt1[:, 0:Q]]
+    fin = 7
+    sl = first[GE]
+
+    def S(i):
+        if i == 0:
+            pe.wait_ge(sem.ldq, 16)
+            pe.wait_ge(sem.ldk, 16)
+        if arr[i]:
+            pe.wait_ge(sem["ka%d" % i], arr[i])
+        pe.matmul(sbank(i), T.qs[:, :], kcols(first[i], nb[i]), True, True).then_inc(sem.sS, 1)
+
+    def TR(i):
+        if i == 0:
+            pe.wait_ge(sem.i2, 1)
+        pe.wait_ge(sem.sE, i + 1)
+        for b in range(nb[i]):
+            pe.transpose(T.ptt0[:, b * Q:(b + 1) * Q], ptcols(first[i] + b, 1), ident).then_inc(sem.sT, 1)
+
+    def PV(i):
+        if i > 0:
+            pe.wait_ge(sem.sA, i)
+            pe.matmul(acc, ident, accs(i), True, False)
+        pe.wait_ge(sem.sP, i + 1)
+        if i == 0:
+            pe.wait_ge(sem.ldv, 16)
+        if arr[i]:
+            pe.wait_ge(sem["va%d" % i], arr[i])
+        for b in range(nb[i]):
+            ins = pe.matmul(acc, pcols(first[i] + b, 1), vcols(first[i] + b), i == 0 and b == 0, b == nb[i] - 1)
+            if b == nb[i] - 1:
+                ins.then_inc(sem.sO, 1)
+
+    S(0)
+    for i in range(GE):
+        if i + 1 < GE:
+            S(i + 1)
+        TR(i)
+        PV(i)
+    for b in range(NL):
+        pe.wait_ge(sem["kl%d" % b], E_DIRECT)
+        pe.matmul(lbank[b], T.qs[:, :], kcols(sl + b, 1), True, True).then_inc(sem.sSL, 1)
+    for b in range(NL):
+        pe.wait_ge(sem.sEL, b + 1)
+        if b >= 2:
+            pe.wait_ge(sem.sPL, b - 1)
+        pe.transpose(lptt[b % 2], ptcols(sl + b, 1), ident).then_inc(sem.sTL, 1)
+        if b == 0:
+            pe.wait_ge(sem.sA, GE)
+            pe.matmul(acc, ident, accs(GE), True, False)
+    for b in range(NL):
+        pe.wait_ge(sem.sPL, b + 1)
+        pe.wait_ge(sem["vl%d" % b], E_DIRECT)
+        ins = pe.matmul(acc, pcols(sl + b, 1), vcols(sl + b), False, b == NL - 1)
+        if b == NL - 1:
+            ins.then_inc(sem.sO, 1)
+
+    def RED(i):
+        ve.wait_ge(sem.sS, i + 1)
+        if i == 0:
+            ve.tensor_reduce(col(T.negm, 0), sbank(0), AxisListType.X, AluOpType.max, negate=True).then_inc(sem.sM, 1)
+            return
+        ve.tensor_reduce(col(T.nm, i), sbank(i), AxisListType.X, AluOpType.max, negate=True).then_inc(sem.sR, 1)
+        ve.wait_ge(sem.sR, i)
+        ve.wait_ge(sem.sM, i)
+        ve.tensor_tensor(col(T.negm, i), col(T.negm, i - 1), col(T.nm, i), AluOpType.min).then_inc(sem.sM, 1)
+
+    def EVAC(i):
+        ve.wait_ge(sem.sO, i)
+        ve.wait_ge(sem.sW, i)
+        ve.tensor_scalar(accs(i), acc, col(T.w, i), None, AluOpType.mult).then_inc(sem.sA, 1)
+
+    def COPY(i):
+        tcount[0] += nb[i]
+        ve.wait_ge(sem.sT, tcount[0])
+        ve.tensor_copy(pcols(first[i], nb[i]), T.ptt0[:, 0:nb[i] * Q]).then_inc(sem.sP, 1)
+
+    def LRUN(i):
+        ve.wait_ge(sem.sE, i + 1)
+        ve.wait_ge(sem.sW, i)
+        if i > 1:
+            ve.wait_ge(sem.sL, i - 1)
+        prev = col(T.l, 0) if i == 1 else col(T.lrun, i - 1)
+        ve.tensor_scalar(col(T.lrun, i), prev, col(T.w, i), col(T.l, i), AluOpType.mult, AluOpType.add).then_inc(sem.sL, 1)
+
+    RED(0)
+    for i in range(GE):
+        if i + 1 < GE:
+            RED(i + 1)
+        if i > 0:
+            EVAC(i)
+        COPY(i)
+        if i > 0:
+            LRUN(i)
+    for b in range(NL):
+        ve.wait_ge(sem.sSL, b + 1)
+        ve.tensor_reduce(col(T.negm, GE + b), lbank[b], AxisListType.X, AluOpType.max, negate=True).then_inc(sem.sRL, 1)
+    ve.wait_ge(sem.sRL, NL)
+    ve.wait_ge(sem.sM, GE)
+    ve.tensor_reduce(col(T.negm, fin), T.negm[0:Q, GE - 1:GE + NL], AxisListType.X, AluOpType.min).then_inc(sem.sM, 1)
+    EVAC(GE)
+    lprev = col(T.l, 0) if GE == 1 else col(T.lrun, GE - 1)
+    for b in range(NL):
+        ve.wait_ge(sem.sTL, b + 1)
+        ve.tensor_copy(pcols(sl + b, 1), lptt[b % 2]).then_inc(sem.sPL, 1)
+        ve.wait_ge(sem.sEL, b + 1)
+        if b == 0:
+            if GE > 1:
+                ve.wait_ge(sem.sL, GE - 1)
+            ve.tensor_scalar(col(T.lt, 0), lprev, col(T.w, GE), col(T.l, GE), AluOpType.mult, AluOpType.add).then_inc(sem.sLL, 1)
+        else:
+            ve.wait_ge(sem.sLL, b)
+            ve.tensor_tensor(col(T.lt, b), col(T.lt, b - 1), col(T.l, GE + b), AluOpType.add).then_inc(sem.sLL, 1)
+    ve.wait_ge(sem.sLL, NL)
+    ve.reciprocal(col(T.r, 0), col(T.lt, NL - 1)).then_inc(sem.sC, 1)
+    ve.wait_ge(sem.sC, 1)
+    ve.wait_ge(sem.sO, G)
+    ve.tensor_scalar(T.ysb[0:Q, :], acc, col(T.r, 0), None, AluOpType.mult).then_inc(sem.sY, 1)
+
+    for i in range(GE):
+        ac.wait_ge(sem.sM, i + 1)
+        ac.activation(ptcols(first[i], nb[i]), sbank(i), Exp, bias=col(T.negm, i), scale=1.0,
+                      accum_out=col(T.l, i)).then_inc(sem.sE, 1)
+        if i > 0:
+            ac.activation(col(T.w, i), col(T.negm, i - 1), Exp, bias=col(T.negm, i), scale=-1.0).then_inc(sem.sW, 1)
+    ac.wait_ge(sem.sM, G)
+    ac.activation(col(T.w, GE), col(T.negm, GE - 1), Exp, bias=col(T.negm, fin), scale=-1.0).then_inc(sem.sW, 1)
+    for b in range(NL):
+        ac.activation(ptcols(sl + b, 1), lbank[b], Exp, bias=col(T.negm, fin), scale=1.0,
+                      accum_out=col(T.l, GE + b)).then_inc(sem.sEL, 1)
+
+    g.sync.wait_ge(sem.sY, 1)
+    g.sync.dma_start(T.y[:, :], T.ysb[0:Q, :]).then_inc(sem.st, 16)
+    g.sync.wait_ge(sem.st, 16)

@@ -6,8 +6,6 @@ MAXL = 3
 E_HOME = 16
 E_DIRECT = 8
 E_FEED = 8
-PASS_K = "rank"
-PASS_V = "rank"
 
 SCRATCH = {
     "qs": ("sbuf", [128, 64], "bfloat16"),
@@ -17,11 +15,12 @@ SCRATCH = {
     "rv": ("sbuf", [128, 128], "bfloat16"),
     "kall": ("sbuf", [128, 2048], "bfloat16"),
     "vall": ("sbuf", [128, 2048], "bfloat16"),
+    "zero": ("sbuf", [128, 64], "bfloat16"),
     "ones": ("sbuf", [128, 64], "bfloat16"),
     "ident": ("sbuf", [128, 64], "bfloat16"),
     "pt": ("sbuf", [128, 2048], "bfloat16"),
     "p": ("sbuf", [128, 1024], "bfloat16"),
-    "accs": ("sbuf", [128, 128 * MAXG], "bfloat16"),
+    "accs": ("sbuf", [128, 128], "bfloat16"),
     "nm": ("sbuf", [128, 8], "float32"),
     "negm": ("sbuf", [128, 8], "float32"),
     "l": ("sbuf", [128, 8], "float32"),
@@ -41,7 +40,7 @@ SCRATCH = {
 }
 SEMAPHORES = (["ka%d" % i for i in range(MAXG)] + ["va%d" % i for i in range(MAXG)] +
               ["kl%d" % i for i in range(MAXL)] + ["vl%d" % i for i in range(MAXL)] +
-              ["ldq", "ldk", "ldv", "rka", "rva", "sent", "i1", "i2",
+              ["ldq", "ldk", "ldv", "rka", "rva", "sent", "i0", "i1", "i2",
                "sS", "sR", "sM", "sE", "sW", "sT", "sP", "sA", "sO", "sL", "sC", "sY", "st",
                "sSL", "sRL", "sEL", "sTL", "sPL", "sLL"])
 
@@ -56,15 +55,10 @@ def _bits(mask, n):
     return out
 
 
-def _passer(T, topo, c, idx, root, direct, mode):
-    if mode == "rank":
-        return [d for d in direct if topo.chip(d) == topo.chip(c)][0]
-    free = [h for h in range(NCORES) if T.rank_of(h) is None and topo.may_write(h, root) and topo.may_write(c, h)]
-    if mode == "chip":
-        return [h for h in free if topo.chip(h) == topo.chip(c) and topo.die(h) == topo.die(c)][0]
-    cand = [h for h in free if topo.mates(topo.chip(h), topo.chip(root))]
-    cand.sort(key=lambda h: topo.die(h) != topo.die(c))
-    return cand[idx]
+def _passer(T, topo, c, root):
+    free = [h for h in range(NCORES) if T.rank_of(h) is None and topo.may_write(h, root) and topo.may_write(c, h)
+            and topo.chip(h) == topo.chip(c) and topo.die(h) == topo.die(c)]
+    return free[0]
 
 
 def _plan(T, topo):
@@ -84,11 +78,10 @@ def _plan(T, topo):
         for i in range(0, len(mem), 4):
             groups.append(mem[i:i + 4])
     groups.append(late)
-    pk, pv = {}, {}
-    for i, c in enumerate(late):
-        pk[c] = _passer(T, topo, c, i, root, direct, PASS_K)
-        pv[c] = _passer(T, topo, c, i, root, direct, PASS_V)
-    return root, groups, late, pk, pv
+    ps = {}
+    for c in late:
+        ps[c] = _passer(T, topo, c, root)
+    return root, groups, late, ps
 
 
 def _write(g, T, topo, src, dst, out_ap, in_ap, rsem, n):
@@ -99,7 +92,7 @@ def _write(g, T, topo, src, dst, out_ap, in_ap, rsem, n):
 
 
 def rank_program(g, core, T, topo):
-    root, groups, late, pk, pv = _plan(T, topo)
+    root, groups, late, ps = _plan(T, topo)
     slot, grp = {}, {}
     for gi, mem in enumerate(groups):
         for c in mem:
@@ -121,11 +114,11 @@ def rank_program(g, core, T, topo):
     if T.rank_of(core) is not None:
         g.sync.dma_start(T.ko[:, :], T.k[:, :]).then_inc(sem.ldk, 16)
         g.scalar.dma_start(T.vo[:, :], T.v[:, :]).then_inc(sem.ldv, 16)
-        if core in pk:
+        if core in ps:
             g.wait_ge(sem.ldk, 16)
-            sent += _write(g, T, topo, core, pk[core], T.rk[:, :], T.ko[:, :], sem.rka, E_FEED)
+            sent += _write(g, T, topo, core, ps[core], T.rk[:, :], T.ko[:, :], sem.rka, E_FEED)
             g.wait_ge(sem.ldv, 16)
-            sent += _write(g, T, topo, core, pv[core], T.rv[:, :], T.vo[:, :], sem.rva, E_FEED)
+            sent += _write(g, T, topo, core, ps[core], T.rv[:, :], T.vo[:, :], sem.rva, E_FEED)
         else:
             n = E_HOME if topo.chip(core) == topo.chip(root) else E_DIRECT
             g.wait_ge(sem.ldk, 16)
@@ -133,10 +126,9 @@ def rank_program(g, core, T, topo):
             g.wait_ge(sem.ldv, 16)
             sent += _write(g, T, topo, core, root, vslot(core), T.vo[:, :], sem["va%d" % grp[core]], n)
     for b, c in enumerate(late):
-        if pk[c] == core:
+        if ps[c] == core:
             g.wait_ge(sem.rka, E_FEED)
             sent += _write(g, T, topo, core, root, kslot(c), T.rk[:, :], sem["kl%d" % b], E_DIRECT)
-        if pv[c] == core:
             g.wait_ge(sem.rva, E_FEED)
             sent += _write(g, T, topo, core, root, vslot(c), T.rv[:, :], sem["vl%d" % b], E_DIRECT)
     if sent:
@@ -148,6 +140,7 @@ def _root(g, core, T, topo, groups, slot):
     G = len(groups)
     GE = G - 1
     Q = 64
+    X = AxisListType.X
     pe, ve, ac = g.tensor, g.vector, g.scalar
     Exp = ActivationFunctionType.Exp
     first = [slot[mem[0]] for mem in groups]
@@ -166,7 +159,9 @@ def _root(g, core, T, topo, groups, slot):
     g.scalar.dma_start(T.kall[:, s0 * 128:(s0 + 1) * 128], T.k[:, :]).then_inc(sem.ldk, 16)
     g.sync.dma_start(T.vall[:, s0 * 128:(s0 + 1) * 128], T.v[:, :]).then_inc(sem.ldv, 16)
 
-    ve.memset(T.ones[0:Q, :], 1.0).then_inc(sem.i1, 1)
+    ve.memset(T.zero[0:Q, :], 0.0).then_inc(sem.i0, 1)
+    ac.wait_ge(sem.i0, 1)
+    ac.activation(T.ones[0:Q, :], T.zero[0:Q, :], Exp).then_inc(sem.i1, 1)
     g.wait_ge(sem.i1, 1)
     g.affine_select(T.ident[0:Q, :], T.ones[0:Q, :], [[-1, Q]], AluOpType.is_equal, 0.0, 0, 1).then_inc(sem.i2, 1)
     ident = T.ident[0:Q, 0:Q]
@@ -189,13 +184,13 @@ def _root(g, core, T, topo, groups, slot):
     def pcols(s, n):
         return T.p[:, s * Q:(s + n) * Q]
 
-    def accs(i):
-        return T.accs[0:Q, i * 128:(i + 1) * 128]
-
     acc = T.acc[0:Q, 0:128]
+    accs = T.accs[0:Q, 0:128]
+    ptt = [T.ptt0, T.ptt1]
     tcount = [0]
     lbank = [T["s%d" % i][0:Q, 0:128] for i in ([GE] + list(range(NL - 1)))]
     lptt = [T.ptt0[:, 0:Q], T.ptt1[:, 0:Q]]
+    ME = GE - 1
     fin = 7
     sl = first[GE]
 
@@ -211,28 +206,29 @@ def _root(g, core, T, topo, groups, slot):
         if i == 0:
             pe.wait_ge(sem.i2, 1)
         pe.wait_ge(sem.sE, i + 1)
+        if i >= 2:
+            pe.wait_ge(sem.sP, i - 1)
         for b in range(nb[i]):
-            pe.transpose(T.ptt0[:, b * Q:(b + 1) * Q], ptcols(first[i] + b, 1), ident).then_inc(sem.sT, 1)
+            pe.transpose(ptt[i % 2][:, b * Q:(b + 1) * Q], ptcols(first[i] + b, 1), ident).then_inc(sem.sT, 1)
 
     def PV(i):
-        if i > 0:
-            pe.wait_ge(sem.sA, i)
-            pe.matmul(acc, ident, accs(i), True, False)
         pe.wait_ge(sem.sP, i + 1)
         if i == 0:
             pe.wait_ge(sem.ldv, 16)
         if arr[i]:
             pe.wait_ge(sem["va%d" % i], arr[i])
         for b in range(nb[i]):
-            ins = pe.matmul(acc, pcols(first[i] + b, 1), vcols(first[i] + b), i == 0 and b == 0, b == nb[i] - 1)
-            if b == nb[i] - 1:
+            end = i == GE - 1 and b == nb[i] - 1
+            ins = pe.matmul(acc, pcols(first[i] + b, 1), vcols(first[i] + b), i == 0 and b == 0, end)
+            if end:
                 ins.then_inc(sem.sO, 1)
 
-    S(0)
+    for i in range(GE):
+        S(i)
+    TR(0)
     for i in range(GE):
         if i + 1 < GE:
-            S(i + 1)
-        TR(i)
+            TR(i + 1)
         PV(i)
     for b in range(NL):
         pe.wait_ge(sem["kl%d" % b], E_DIRECT)
@@ -243,8 +239,8 @@ def _root(g, core, T, topo, groups, slot):
             pe.wait_ge(sem.sPL, b - 1)
         pe.transpose(lptt[b % 2], ptcols(sl + b, 1), ident).then_inc(sem.sTL, 1)
         if b == 0:
-            pe.wait_ge(sem.sA, GE)
-            pe.matmul(acc, ident, accs(GE), True, False)
+            pe.wait_ge(sem.sA, 1)
+            pe.matmul(acc, ident, accs, True, False)
     for b in range(NL):
         pe.wait_ge(sem.sPL, b + 1)
         pe.wait_ge(sem["vl%d" % b], E_DIRECT)
@@ -252,76 +248,49 @@ def _root(g, core, T, topo, groups, slot):
         if b == NL - 1:
             ins.then_inc(sem.sO, 1)
 
-    def RED(i):
+    for i in range(GE):
         ve.wait_ge(sem.sS, i + 1)
-        if i == 0:
-            ve.tensor_reduce(col(T.negm, 0), sbank(0), AxisListType.X, AluOpType.max, negate=True).then_inc(sem.sM, 1)
-            return
-        ve.tensor_reduce(col(T.nm, i), sbank(i), AxisListType.X, AluOpType.max, negate=True).then_inc(sem.sR, 1)
-        ve.wait_ge(sem.sR, i)
-        ve.wait_ge(sem.sM, i)
-        ve.tensor_tensor(col(T.negm, i), col(T.negm, i - 1), col(T.nm, i), AluOpType.min).then_inc(sem.sM, 1)
-
-    def EVAC(i):
-        ve.wait_ge(sem.sO, i)
-        ve.wait_ge(sem.sW, i)
-        ve.tensor_scalar(accs(i), acc, col(T.w, i), None, AluOpType.mult).then_inc(sem.sA, 1)
-
-    def COPY(i):
+        ve.tensor_reduce(col(T.nm, i), sbank(i), X, AluOpType.max, negate=True).then_inc(sem.sR, 1)
+    ve.wait_ge(sem.sR, GE)
+    ve.tensor_reduce(col(T.negm, ME), T.nm[0:Q, 0:GE], X, AluOpType.min).then_inc(sem.sM, 1)
+    for i in range(GE):
         tcount[0] += nb[i]
         ve.wait_ge(sem.sT, tcount[0])
-        ve.tensor_copy(pcols(first[i], nb[i]), T.ptt0[:, 0:nb[i] * Q]).then_inc(sem.sP, 1)
-
-    def LRUN(i):
-        ve.wait_ge(sem.sE, i + 1)
-        ve.wait_ge(sem.sW, i)
-        if i > 1:
-            ve.wait_ge(sem.sL, i - 1)
-        prev = col(T.l, 0) if i == 1 else col(T.lrun, i - 1)
-        ve.tensor_scalar(col(T.lrun, i), prev, col(T.w, i), col(T.l, i), AluOpType.mult, AluOpType.add).then_inc(sem.sL, 1)
-
-    RED(0)
-    for i in range(GE):
-        if i + 1 < GE:
-            RED(i + 1)
-        if i > 0:
-            EVAC(i)
-        COPY(i)
-        if i > 0:
-            LRUN(i)
+        ve.tensor_copy(pcols(first[i], nb[i]), ptt[i % 2][:, 0:nb[i] * Q]).then_inc(sem.sP, 1)
     for b in range(NL):
         ve.wait_ge(sem.sSL, b + 1)
-        ve.tensor_reduce(col(T.negm, GE + b), lbank[b], AxisListType.X, AluOpType.max, negate=True).then_inc(sem.sRL, 1)
+        ve.tensor_reduce(col(T.negm, GE + b), lbank[b], X, AluOpType.max, negate=True).then_inc(sem.sRL, 1)
     ve.wait_ge(sem.sRL, NL)
-    ve.wait_ge(sem.sM, GE)
-    ve.tensor_reduce(col(T.negm, fin), T.negm[0:Q, GE - 1:GE + NL], AxisListType.X, AluOpType.min).then_inc(sem.sM, 1)
-    EVAC(GE)
-    lprev = col(T.l, 0) if GE == 1 else col(T.lrun, GE - 1)
+    ve.wait_ge(sem.sM, 1)
+    ve.tensor_reduce(col(T.negm, fin), T.negm[0:Q, ME:GE + NL], X, AluOpType.min).then_inc(sem.sM, 1)
+    ve.wait_ge(sem.sO, 1)
+    ve.wait_ge(sem.sW, 1)
+    ve.tensor_scalar(accs, acc, col(T.w, 0), None, AluOpType.mult).then_inc(sem.sA, 1)
+    ve.wait_ge(sem.sE, GE)
+    ve.tensor_reduce(col(T.lrun, 0), T.l[0:Q, 0:GE], X, AluOpType.add).then_inc(sem.sL, 1)
     for b in range(NL):
         ve.wait_ge(sem.sTL, b + 1)
         ve.tensor_copy(pcols(sl + b, 1), lptt[b % 2]).then_inc(sem.sPL, 1)
         ve.wait_ge(sem.sEL, b + 1)
         if b == 0:
-            if GE > 1:
-                ve.wait_ge(sem.sL, GE - 1)
-            ve.tensor_scalar(col(T.lt, 0), lprev, col(T.w, GE), col(T.l, GE), AluOpType.mult, AluOpType.add).then_inc(sem.sLL, 1)
+            ve.wait_ge(sem.sL, 1)
+            ve.tensor_scalar(col(T.lt, 0), col(T.lrun, 0), col(T.w, 0), col(T.l, GE), AluOpType.mult,
+                             AluOpType.add).then_inc(sem.sLL, 1)
         else:
             ve.wait_ge(sem.sLL, b)
             ve.tensor_tensor(col(T.lt, b), col(T.lt, b - 1), col(T.l, GE + b), AluOpType.add).then_inc(sem.sLL, 1)
     ve.wait_ge(sem.sLL, NL)
     ve.reciprocal(col(T.r, 0), col(T.lt, NL - 1)).then_inc(sem.sC, 1)
     ve.wait_ge(sem.sC, 1)
-    ve.wait_ge(sem.sO, G)
+    ve.wait_ge(sem.sO, 2)
     ve.tensor_scalar(T.ysb[0:Q, :], acc, col(T.r, 0), None, AluOpType.mult).then_inc(sem.sY, 1)
 
+    ac.wait_ge(sem.sM, 1)
     for i in range(GE):
-        ac.wait_ge(sem.sM, i + 1)
-        ac.activation(ptcols(first[i], nb[i]), sbank(i), Exp, bias=col(T.negm, i), scale=1.0,
+        ac.activation(ptcols(first[i], nb[i]), sbank(i), Exp, bias=col(T.negm, ME), scale=1.0,
                       accum_out=col(T.l, i)).then_inc(sem.sE, 1)
-        if i > 0:
-            ac.activation(col(T.w, i), col(T.negm, i - 1), Exp, bias=col(T.negm, i), scale=-1.0).then_inc(sem.sW, 1)
-    ac.wait_ge(sem.sM, G)
-    ac.activation(col(T.w, GE), col(T.negm, GE - 1), Exp, bias=col(T.negm, fin), scale=-1.0).then_inc(sem.sW, 1)
+    ac.wait_ge(sem.sM, 2)
+    ac.activation(col(T.w, 0), col(T.negm, ME), Exp, bias=col(T.negm, fin), scale=-1.0).then_inc(sem.sW, 1)
     for b in range(NL):
         ac.activation(ptcols(sl + b, 1), lbank[b], Exp, bias=col(T.negm, fin), scale=1.0,
                       accum_out=col(T.l, GE + b)).then_inc(sem.sEL, 1)

@@ -9,18 +9,19 @@ E_FEED = 8
 
 SCRATCH = {
     "qs": ("sbuf", [128, 64], "bfloat16"),
-    "ko": ("sbuf", [128, 128], "bfloat16"),
-    "vo": ("sbuf", [128, 128], "bfloat16"),
-    "rk": ("sbuf", [128, 128], "bfloat16"),
-    "rv": ("sbuf", [128, 128], "bfloat16"),
+    "ko": ("dram", [128, 128], "bfloat16"),
+    "vo": ("dram", [128, 128], "bfloat16"),
+    "rk": ("dram", [128, 128], "bfloat16"),
+    "rv": ("dram", [128, 128], "bfloat16"),
     "kall": ("sbuf", [128, 2048], "bfloat16"),
     "vall": ("sbuf", [128, 2048], "bfloat16"),
-    "zero": ("sbuf", [128, 64], "bfloat16"),
-    "ones": ("sbuf", [128, 64], "bfloat16"),
-    "ident": ("sbuf", [128, 64], "bfloat16"),
+    "zero": ("sbuf", [128, 128], "bfloat16"),
+    "ones": ("sbuf", [128, 128], "bfloat16"),
+    "ident": ("sbuf", [128, 128], "bfloat16"),
     "pt": ("sbuf", [128, 2048], "bfloat16"),
     "p": ("sbuf", [128, 1024], "bfloat16"),
     "accs": ("sbuf", [128, 128], "bfloat16"),
+    "accts": ("sbuf", [128, 64], "bfloat16"),
     "nm": ("sbuf", [128, 8], "float32"),
     "negm": ("sbuf", [128, 8], "float32"),
     "l": ("sbuf", [128, 8], "float32"),
@@ -42,7 +43,7 @@ SEMAPHORES = (["ka%d" % i for i in range(MAXG)] + ["va%d" % i for i in range(MAX
               ["kl%d" % i for i in range(MAXL)] + ["vl%d" % i for i in range(MAXL)] +
               ["ldq", "ldk", "ldv", "rka", "rva", "sent", "i0", "i1", "i2",
                "sS", "sR", "sM", "sE", "sW", "sT", "sP", "sA", "sO", "sL", "sC", "sY", "st",
-               "sSL", "sRL", "sEL", "sTL", "sPL", "sLL"])
+               "sSL", "sRL", "sEL", "sTL", "sPL", "sLL", "sX", "sB"])
 
 
 def _bits(mask, n):
@@ -55,10 +56,12 @@ def _bits(mask, n):
     return out
 
 
-def _passer(T, topo, c, root):
-    free = [h for h in range(NCORES) if T.rank_of(h) is None and topo.may_write(h, root) and topo.may_write(c, h)
-            and topo.chip(h) == topo.chip(c) and topo.die(h) == topo.die(c)]
-    return free[0]
+def _passers(T, topo, c, root):
+    near = [h for h in range(NCORES) if h != c and topo.chip(h) == topo.chip(c) and topo.may_write(h, root)
+            and topo.may_write(c, h)]
+    own = [h for h in near if T.rank_of(h) is not None]
+    free = [h for h in near if T.rank_of(h) is None and topo.die(h) == topo.die(c)]
+    return own[0], free[0]
 
 
 def _plan(T, topo):
@@ -78,10 +81,10 @@ def _plan(T, topo):
         for i in range(0, len(mem), 4):
             groups.append(mem[i:i + 4])
     groups.append(late)
-    ps = {}
+    pk, pv = {}, {}
     for c in late:
-        ps[c] = _passer(T, topo, c, root)
-    return root, groups, late, ps
+        pk[c], pv[c] = _passers(T, topo, c, root)
+    return root, groups, late, pk, pv
 
 
 def _write(g, T, topo, src, dst, out_ap, in_ap, rsem, n):
@@ -92,7 +95,7 @@ def _write(g, T, topo, src, dst, out_ap, in_ap, rsem, n):
 
 
 def rank_program(g, core, T, topo):
-    root, groups, late, ps = _plan(T, topo)
+    root, groups, late, pk, pv = _plan(T, topo)
     slot, grp = {}, {}
     for gi, mem in enumerate(groups):
         for c in mem:
@@ -114,21 +117,23 @@ def rank_program(g, core, T, topo):
     if T.rank_of(core) is not None:
         g.sync.dma_start(T.ko[:, :], T.k[:, :]).then_inc(sem.ldk, 16)
         g.scalar.dma_start(T.vo[:, :], T.v[:, :]).then_inc(sem.ldv, 16)
-        if core in ps:
+        if core in pk:
             g.wait_ge(sem.ldk, 16)
-            sent += _write(g, T, topo, core, ps[core], T.rk[:, :], T.ko[:, :], sem.rka, E_FEED)
+            sent += _write(g, T, topo, core, pk[core], T.rk[:, :], T.ko[:, :], sem.rka, E_FEED)
             g.wait_ge(sem.ldv, 16)
-            sent += _write(g, T, topo, core, ps[core], T.rv[:, :], T.vo[:, :], sem.rva, E_FEED)
+            sent += _write(g, T, topo, core, pv[core], T.rv[:, :], T.vo[:, :], sem.rva, E_FEED)
         else:
             n = E_HOME if topo.chip(core) == topo.chip(root) else E_DIRECT
             g.wait_ge(sem.ldk, 16)
             sent += _write(g, T, topo, core, root, kslot(core), T.ko[:, :], sem["ka%d" % grp[core]], n)
+            for b, c in enumerate(late):
+                if pk[c] == core:
+                    g.wait_ge(sem.rka, E_FEED)
+                    sent += _write(g, T, topo, core, root, kslot(c), T.rk[:, :], sem["kl%d" % b], E_DIRECT)
             g.wait_ge(sem.ldv, 16)
             sent += _write(g, T, topo, core, root, vslot(core), T.vo[:, :], sem["va%d" % grp[core]], n)
     for b, c in enumerate(late):
-        if ps[c] == core:
-            g.wait_ge(sem.rka, E_FEED)
-            sent += _write(g, T, topo, core, root, kslot(c), T.rk[:, :], sem["kl%d" % b], E_DIRECT)
+        if pv[c] == core:
             g.wait_ge(sem.rva, E_FEED)
             sent += _write(g, T, topo, core, root, vslot(c), T.rv[:, :], sem["vl%d" % b], E_DIRECT)
     if sent:
@@ -146,6 +151,7 @@ def _root(g, core, T, topo, groups, slot):
     first = [slot[mem[0]] for mem in groups]
     nb = [len(mem) for mem in groups]
     NL = nb[GE]
+    HOIST = 1
     arr = []
     for mem in groups[:GE]:
         a = 0
@@ -159,15 +165,18 @@ def _root(g, core, T, topo, groups, slot):
     g.scalar.dma_start(T.kall[:, s0 * 128:(s0 + 1) * 128], T.k[:, :]).then_inc(sem.ldk, 16)
     g.sync.dma_start(T.vall[:, s0 * 128:(s0 + 1) * 128], T.v[:, :]).then_inc(sem.ldv, 16)
 
-    ve.memset(T.zero[0:Q, :], 0.0).then_inc(sem.i0, 1)
+    ve.memset(T.zero[:, :], 0.0).then_inc(sem.i0, 1)
     ac.wait_ge(sem.i0, 1)
-    ac.activation(T.ones[0:Q, :], T.zero[0:Q, :], Exp).then_inc(sem.i1, 1)
+    ac.activation(T.ones[:, :], T.zero[:, :], Exp).then_inc(sem.i1, 1)
     g.wait_ge(sem.i1, 1)
-    g.affine_select(T.ident[0:Q, :], T.ones[0:Q, :], [[-1, Q]], AluOpType.is_equal, 0.0, 0, 1).then_inc(sem.i2, 1)
+    g.affine_select(T.ident[:, :], T.ones[:, :], [[-1, 128]], AluOpType.is_equal, 0.0, 0, 1).then_inc(sem.i2, 1)
     ident = T.ident[0:Q, 0:Q]
 
     def sbank(i):
         return T["s%d" % i][0:Q, 0:nb[i] * 128]
+
+    def lcol(b):
+        return T["s%d" % GE][0:Q, b * 128:(b + 1) * 128]
 
     def col(t, i):
         return t[0:Q, i:i + 1]
@@ -184,11 +193,12 @@ def _root(g, core, T, topo, groups, slot):
     def pcols(s, n):
         return T.p[:, s * Q:(s + n) * Q]
 
-    acc = T.acc[0:Q, 0:128]
+    acc = T.s0[0:Q, 0:128]
+    accT = T.acc[:, 0:Q]
+    eT = T.acc[0:Q, 128:256]
     accs = T.accs[0:Q, 0:128]
     ptt = [T.ptt0, T.ptt1]
     tcount = [0]
-    lbank = [T["s%d" % i][0:Q, 0:128] for i in ([GE] + list(range(NL - 1)))]
     lptt = [T.ptt0[:, 0:Q], T.ptt1[:, 0:Q]]
     ME = GE - 1
     fin = 7
@@ -219,7 +229,7 @@ def _root(g, core, T, topo, groups, slot):
             pe.wait_ge(sem["va%d" % i], arr[i])
         for b in range(nb[i]):
             end = i == GE - 1 and b == nb[i] - 1
-            ins = pe.matmul(acc, pcols(first[i] + b, 1), vcols(first[i] + b), i == 0 and b == 0, end)
+            ins = pe.matmul(accT, vcols(first[i] + b), pcols(first[i] + b, 1), i == 0 and b == 0, end)
             if end:
                 ins.then_inc(sem.sO, 1)
 
@@ -230,23 +240,24 @@ def _root(g, core, T, topo, groups, slot):
         if i + 1 < GE:
             TR(i + 1)
         PV(i)
-    for b in range(NL):
-        pe.wait_ge(sem["kl%d" % b], E_DIRECT)
-        pe.matmul(lbank[b], T.qs[:, :], kcols(sl + b, 1), True, True).then_inc(sem.sSL, 1)
+        if i + 1 == HOIST:
+            for b in range(NL):
+                pe.wait_ge(sem["kl%d" % b], E_DIRECT)
+                pe.matmul(lcol(b), T.qs[:, :], kcols(sl + b, 1), True, True).then_inc(sem.sSL, 1)
     for b in range(NL):
         pe.wait_ge(sem.sEL, b + 1)
         if b >= 2:
             pe.wait_ge(sem.sPL, b - 1)
         pe.transpose(lptt[b % 2], ptcols(sl + b, 1), ident).then_inc(sem.sTL, 1)
-        if b == 0:
-            pe.wait_ge(sem.sA, 1)
-            pe.matmul(acc, ident, accs, True, False)
+        if b == min(1, NL - 1):
+            pe.wait_ge(sem.sX, 1)
+            pe.matmul(eT, T.accts[:, :], T.ident[:, :], True, True).then_inc(sem.sB, 1)
     for b in range(NL):
         pe.wait_ge(sem.sPL, b + 1)
         pe.wait_ge(sem["vl%d" % b], E_DIRECT)
-        ins = pe.matmul(acc, pcols(sl + b, 1), vcols(sl + b), False, b == NL - 1)
-        if b == NL - 1:
-            ins.then_inc(sem.sO, 1)
+        pe.matmul(acc, pcols(sl + b, 1), vcols(sl + b), b == 0, False)
+    pe.wait_ge(sem.sA, 1)
+    pe.matmul(acc, ident, accs, False, True).then_inc(sem.sO, 1)
 
     for i in range(GE):
         ve.wait_ge(sem.sS, i + 1)
@@ -257,23 +268,28 @@ def _root(g, core, T, topo, groups, slot):
         tcount[0] += nb[i]
         ve.wait_ge(sem.sT, tcount[0])
         ve.tensor_copy(pcols(first[i], nb[i]), ptt[i % 2][:, 0:nb[i] * Q]).then_inc(sem.sP, 1)
-    for b in range(NL):
-        ve.wait_ge(sem.sSL, b + 1)
-        ve.tensor_reduce(col(T.negm, GE + b), lbank[b], X, AluOpType.max, negate=True).then_inc(sem.sRL, 1)
-    ve.wait_ge(sem.sRL, NL)
-    ve.wait_ge(sem.sM, 1)
-    ve.tensor_reduce(col(T.negm, fin), T.negm[0:Q, ME:GE + NL], X, AluOpType.min).then_inc(sem.sM, 1)
+        if i == HOIST:
+            ve.wait_ge(sem.sSL, NL)
+            ve.tensor_reduce(col(T.negm, GE), T["s%d" % GE][0:Q, 0:NL * 128], X, AluOpType.max,
+                             negate=True).then_inc(sem.sRL, 1)
+            ve.wait_ge(sem.sRL, 1)
+            ve.wait_ge(sem.sM, 1)
+            ve.tensor_reduce(col(T.negm, fin), T.negm[0:Q, ME:GE + 1], X, AluOpType.min).then_inc(sem.sM, 1)
     ve.wait_ge(sem.sO, 1)
-    ve.wait_ge(sem.sW, 1)
-    ve.tensor_scalar(accs, acc, col(T.w, 0), None, AluOpType.mult).then_inc(sem.sA, 1)
+    ve.tensor_copy(T.accts[:, :], accT).then_inc(sem.sX, 1)
     ve.wait_ge(sem.sE, GE)
     ve.tensor_reduce(col(T.lrun, 0), T.l[0:Q, 0:GE], X, AluOpType.add).then_inc(sem.sL, 1)
     for b in range(NL):
+        if b == NL - 1:
+            ve.wait_ge(sem.sB, 1)
+            ve.wait_ge(sem.sW, 1)
+            ve.tensor_scalar(accs, eT, col(T.w, 0), None, AluOpType.mult).then_inc(sem.sA, 1)
         ve.wait_ge(sem.sTL, b + 1)
         ve.tensor_copy(pcols(sl + b, 1), lptt[b % 2]).then_inc(sem.sPL, 1)
         ve.wait_ge(sem.sEL, b + 1)
         if b == 0:
             ve.wait_ge(sem.sL, 1)
+            ve.wait_ge(sem.sW, 1)
             ve.tensor_scalar(col(T.lt, 0), col(T.lrun, 0), col(T.w, 0), col(T.l, GE), AluOpType.mult,
                              AluOpType.add).then_inc(sem.sLL, 1)
         else:
@@ -292,7 +308,7 @@ def _root(g, core, T, topo, groups, slot):
     ac.wait_ge(sem.sM, 2)
     ac.activation(col(T.w, 0), col(T.negm, ME), Exp, bias=col(T.negm, fin), scale=-1.0).then_inc(sem.sW, 1)
     for b in range(NL):
-        ac.activation(ptcols(sl + b, 1), lbank[b], Exp, bias=col(T.negm, fin), scale=1.0,
+        ac.activation(ptcols(sl + b, 1), lcol(b), Exp, bias=col(T.negm, fin), scale=1.0,
                       accum_out=col(T.l, GE + b)).then_inc(sem.sEL, 1)
 
     g.sync.wait_ge(sem.sY, 1)

from concourse.mybir import AluOpType, AxisListType, ActivationFunctionType

NCORES = 128
MAXG = 5
MAXL = 3
E_HOME = 16
E_DIRECT = 8
E_FEED = 8

SCRATCH = {
    "qs": ("sbuf", [128, 64], "bfloat16"),
    "ko": ("dram", [128, 128], "bfloat16"),
    "vo": ("dram", [128, 128], "bfloat16"),
    "rk": ("dram", [128, 128], "bfloat16"),
    "rv": ("dram", [128, 128], "bfloat16"),
    "kall": ("sbuf", [128, 2048], "bfloat16"),
    "vall": ("sbuf", [128, 2048], "bfloat16"),
    "zero": ("sbuf", [128, 128], "bfloat16"),
    "ones": ("sbuf", [128, 128], "bfloat16"),
    "ident": ("sbuf", [128, 128], "bfloat16"),
    "pt": ("sbuf", [128, 2048], "bfloat16"),
    "p": ("sbuf", [128, 1024], "bfloat16"),
    "accs": ("sbuf", [128, 128], "bfloat16"),
    "accts": ("sbuf", [128, 64], "bfloat16"),
    "nm": ("sbuf", [128, 8], "float32"),
    "negm": ("sbuf", [128, 8], "float32"),
    "l": ("sbuf", [128, 8], "float32"),
    "w": ("sbuf", [128, 8], "float32"),
    "lrun": ("sbuf", [128, 8], "float32"),
    "lt": ("sbuf", [128, 8], "float32"),
    "r": ("sbuf", [128, 8], "float32"),
    "ysb": ("sbuf", [128, 128], "bfloat16"),
    "s0": ("psum", [128, 512], "float32"),
    "s1": ("psum", [128, 512], "float32"),
    "s2": ("psum", [128, 512], "float32"),
    "s3": ("psum", [128, 512], "float32"),
    "s4": ("psum", [128, 512], "float32"),
    "ptt0": ("psum", [128, 1024], "bfloat16"),
    "ptt1": ("psum", [128, 1024], "bfloat16"),
    "acc": ("psum", [128, 512], "float32"),
}
SEMAPHORES = (["ka%d" % i for i in range(MAXG)] + ["va%d" % i for i in range(MAXG)] +
              ["kl%d" % i for i in range(MAXL)] + ["vl%d" % i for i in range(MAXL)] +
              ["ldq", "ldk", "ldv", "rka", "rva", "sent", "i0", "i1", "i2",
               "sS", "sR", "sM", "sE", "sW", "sT", "sP", "sA", "sO", "sL", "sC", "sY", "st",
               "sSL", "sRL", "sEL", "sTL", "sPL", "sLL", "sX", "sB"])


def _bits(mask, n):
    out, k, b = 0, 0, 0
    while k < n:
        if (mask >> b) & 1:
            out |= 1 << b
            k += 1
        b += 1
    return out


def _passers(T, topo, c, root):
    near = [h for h in range(NCORES) if h != c and topo.chip(h) == topo.chip(c) and topo.may_write(h, root)
            and topo.may_write(c, h)]
    own = [h for h in near if T.rank_of(h) is not None]
    free = [h for h in near if T.rank_of(h) is None and topo.die(h) == topo.die(c)]
    return own[0], free[0]


def _plan(T, topo):
    cores = list(T.cores)
    root = cores[T.root]
    rc = topo.chip(root)
    home = [root] + [c for c in cores if topo.chip(c) == rc and c != root]
    direct = [c for c in cores if topo.chip(c) != rc and topo.may_write(c, root)]
    late = [c for c in cores if topo.chip(c) != rc and not topo.may_write(c, root)]

    def way(c):
        return (topo.die(c) != topo.die(root), not topo.same_plane(topo.chip(c), rc))

    groups = [home]
    for key in sorted(set(way(c) for c in direct)):
        mem = [c for c in direct if way(c) == key]
        for i in range(0, len(mem), 4):
            groups.append(mem[i:i + 4])
    groups.append(late)
    pk, pv = {}, {}
    for c in late:
        pk[c], pv[c] = _passers(T, topo, c, root)
    return root, groups, late, pk, pv


def _write(g, T, topo, src, dst, out_ap, in_ap, rsem, n):
    rid, pid, _ = topo.addr(dst)
    g.remote_dma(out_ap, in_ap, remote_sem=rsem, local_sem=T.sem.sent, pid=pid, routing_id=rid,
                 dma_engine_mask=_bits(topo.mask(src, dst), n))
    return n


def rank_program(g, core, T, topo):
    root, groups, late, pk, pv = _plan(T, topo)
    slot, grp = {}, {}
    for gi, mem in enumerate(groups):
        for c in mem:
            grp[c] = gi
            slot[c] = len(slot)
    if core == root:
        _root(g, core, T, topo, groups, slot)
        return

    sem = T.sem
    sent = 0

    def kslot(c):
        return T.kall[:, slot[c] * 128:(slot[c] + 1) * 128]

    def vslot(c):
        return T.vall[:, slot[c] * 128:(slot[c] + 1) * 128]

    if T.rank_of(core) is not None:
        g.sync.dma_start(T.ko[:, :], T.k[:, :]).then_inc(sem.ldk, 16)
        g.scalar.dma_start(T.vo[:, :], T.v[:, :]).then_inc(sem.ldv, 16)
        if core in pk:
            g.wait_ge(sem.ldk, 16)
            sent += _write(g, T, topo, core, pk[core], T.rk[:, :], T.ko[:, :], sem.rka, E_FEED)
            g.wait_ge(sem.ldv, 16)
            sent += _write(g, T, topo, core, pv[core], T.rv[:, :], T.vo[:, :], sem.rva, E_FEED)
        else:
            n = E_HOME if topo.chip(core) == topo.chip(root) else E_DIRECT
            g.wait_ge(sem.ldk, 16)
            sent += _write(g, T, topo, core, root, kslot(core), T.ko[:, :], sem["ka%d" % grp[core]], n)
            for b, c in enumerate(late):
                if pk[c] == core:
                    g.wait_ge(sem.rka, E_FEED)
                    sent += _write(g, T, topo, core, root, kslot(c), T.rk[:, :], sem["kl%d" % b], E_DIRECT)
            g.wait_ge(sem.ldv, 16)
            sent += _write(g, T, topo, core, root, vslot(core), T.vo[:, :], sem["va%d" % grp[core]], n)
    for b, c in enumerate(late):
        if pv[c] == core:
            g.wait_ge(sem.rva, E_FEED)
            sent += _write(g, T, topo, core, root, vslot(c), T.rv[:, :], sem["vl%d" % b], E_DIRECT)
    if sent:
        g.wait_ge(sem.sent, sent)


def _root(g, core, T, topo, groups, slot):
    sem = T.sem
    G = len(groups)
    GE = G - 1
    Q = 64
    X = AxisListType.X
    pe, ve, ac = g.tensor, g.vector, g.scalar
    Exp = ActivationFunctionType.Exp
    first = [slot[mem[0]] for mem in groups]
    nb = [len(mem) for mem in groups]
    NL = nb[GE]
    HOIST = 1
    arr = []
    for mem in groups[:GE]:
        a = 0
        for c in mem:
            if c != core:
                a += E_HOME if topo.chip(c) == topo.chip(core) else E_DIRECT
        arr.append(a)

    s0 = slot[core]
    g.sync.dma_start(T.qs[:, :], T.q[:, :]).then_inc(sem.ldq, 16)
    g.scalar.dma_start(T.kall[:, s0 * 128:(s0 + 1) * 128], T.k[:, :]).then_inc(sem.ldk, 16)
    g.sync.dma_start(T.vall[:, s0 * 128:(s0 + 1) * 128], T.v[:, :]).then_inc(sem.ldv, 16)

    ve.memset(T.zero[:, :], 0.0).then_inc(sem.i0, 1)
    ac.wait_ge(sem.i0, 1)
    ac.activation(T.ones[:, :], T.zero[:, :], Exp).then_inc(sem.i1, 1)
    g.wait_ge(sem.i1, 1)
    g.affine_select(T.ident[:, :], T.ones[:, :], [[-1, 128]], AluOpType.is_equal, 0.0, 0, 1).then_inc(sem.i2, 1)
    ident = T.ident[0:Q, 0:Q]

    def sbank(i):
        return T["s%d" % i][0:Q, 0:nb[i] * 128]

    def lcol(b):
        return T["s%d" % GE][0:Q, b * 128:(b + 1) * 128]

    def col(t, i):
        return t[0:Q, i:i + 1]

    def kcols(s, n):
        return T.kall[:, s * 128:(s + n) * 128]

    def vcols(s):
        return T.vall[:, s * 128:(s + 1) * 128]

    def ptcols(s, n):
        return T.pt[0:Q, s * 128:(s + n) * 128]

    def pcols(s, n):
        return T.p[:, s * Q:(s + n) * Q]

    acc = T.s0[0:Q, 0:128]
    accT = T.acc[:, 0:Q]
    eT = T.acc[0:Q, 128:256]
    accs = T.accs[0:Q, 0:128]
    ptt = [T.ptt0, T.ptt1]
    tcount = [0]
    lptt = [T.ptt0[:, 0:Q], T.ptt1[:, 0:Q]]
    ME = GE - 1
    fin = 7
    sl = first[GE]

    def S(i):
        if i == 0:
            pe.wait_ge(sem.ldq, 16)
            pe.wait_ge(sem.ldk, 16)
        if arr[i]:
            pe.wait_ge(sem["ka%d" % i], arr[i])
        pe.matmul(sbank(i), T.qs[:, :], kcols(first[i], nb[i]), True, True).then_inc(sem.sS, 1)

    def TR(i):
        if i == 0:
            pe.wait_ge(sem.i2, 1)
        pe.wait_ge(sem.sE, i + 1)
        if i >= 2:
            pe.wait_ge(sem.sP, i - 1)
        for b in range(nb[i]):
            pe.transpose(ptt[i % 2][:, b * Q:(b + 1) * Q], ptcols(first[i] + b, 1), ident).then_inc(sem.sT, 1)

    def PV(i):
        pe.wait_ge(sem.sP, i + 1)
        if i == 0:
            pe.wait_ge(sem.ldv, 16)
        if arr[i]:
            pe.wait_ge(sem["va%d" % i], arr[i])
        for b in range(nb[i]):
            end = i == GE - 1 and b == nb[i] - 1
            ins = pe.matmul(accT, vcols(first[i] + b), pcols(first[i] + b, 1), i == 0 and b == 0, end)
            if end:
                ins.then_inc(sem.sO, 1)

    for i in range(GE):
        S(i)
    TR(0)
    for i in range(GE):
        if i + 1 < GE:
            TR(i + 1)
        PV(i)
        if i + 1 == HOIST:
            for b in range(NL):
                pe.wait_ge(sem["kl%d" % b], E_DIRECT)
                pe.matmul(lcol(b), T.qs[:, :], kcols(sl + b, 1), True, True).then_inc(sem.sSL, 1)
    for b in range(NL):
        pe.wait_ge(sem.sEL, b + 1)
        if b >= 2:
            pe.wait_ge(sem.sPL, b - 1)
        pe.transpose(lptt[b % 2], ptcols(sl + b, 1), ident).then_inc(sem.sTL, 1)
        if b == min(1, NL - 1):
            pe.wait_ge(sem.sX, 1)
            pe.matmul(eT, T.accts[:, :], T.ident[:, :], True, True).then_inc(sem.sB, 1)
    for b in range(NL):
        pe.wait_ge(sem.sPL, b + 1)
        pe.wait_ge(sem["vl%d" % b], E_DIRECT)
        pe.matmul(acc, pcols(sl + b, 1), vcols(sl + b), b == 0, False)
    pe.wait_ge(sem.sA, 1)
    pe.matmul(acc, ident, accs, False, True).then_inc(sem.sO, 1)

    for i in range(GE):
        ve.wait_ge(sem.sS, i + 1)
        ve.tensor_reduce(col(T.nm, i), sbank(i), X, AluOpType.max, negate=True).then_inc(sem.sR, 1)
    ve.wait_ge(sem.sR, GE)
    ve.tensor_reduce(col(T.negm, ME), T.nm[0:Q, 0:GE], X, AluOpType.min).then_inc(sem.sM, 1)
    for i in range(GE):
        tcount[0] += nb[i]
        ve.wait_ge(sem.sT, tcount[0])
        ve.tensor_copy(pcols(first[i], nb[i]), ptt[i % 2][:, 0:nb[i] * Q]).then_inc(sem.sP, 1)
        if i == HOIST:
            ve.wait_ge(sem.sSL, NL)
            ve.tensor_reduce(col(T.negm, GE), T["s%d" % GE][0:Q, 0:NL * 128], X, AluOpType.max,
                             negate=True).then_inc(sem.sRL, 1)
            ve.wait_ge(sem.sRL, 1)
            ve.wait_ge(sem.sM, 1)
            ve.tensor_reduce(col(T.negm, fin), T.negm[0:Q, ME:GE + 1], X, AluOpType.min).then_inc(sem.sM, 1)
    ve.wait_ge(sem.sO, 1)
    ve.tensor_copy(T.accts[:, :], accT).then_inc(sem.sX, 1)
    ve.wait_ge(sem.sE, GE)
    ve.tensor_reduce(col(T.lrun, 0), T.l[0:Q, 0:GE], X, AluOpType.add).then_inc(sem.sL, 1)
    for b in range(NL):
        if b == NL - 1:
            ve.wait_ge(sem.sB, 1)
            ve.wait_ge(sem.sW, 1)
            ve.tensor_scalar(accs, eT, col(T.w, 0), None, AluOpType.mult).then_inc(sem.sA, 1)
        ve.wait_ge(sem.sTL, b + 1)
        ve.tensor_copy(pcols(sl + b, 1), lptt[b % 2]).then_inc(sem.sPL, 1)
        ve.wait_ge(sem.sEL, b + 1)
        if b == 0:
            ve.wait_ge(sem.sL, 1)
            ve.wait_ge(sem.sW, 1)
            ve.tensor_scalar(col(T.lt, 0), col(T.lrun, 0), col(T.w, 0), col(T.l, GE), AluOpType.mult,
                             AluOpType.add).then_inc(sem.sLL, 1)
        else:
            ve.wait_ge(sem.sLL, b)
            ve.tensor_tensor(col(T.lt, b), col(T.lt, b - 1), col(T.l, GE + b), AluOpType.add).then_inc(sem.sLL, 1)
    ve.wait_ge(sem.sLL, NL)
    ve.reciprocal(col(T.r, 0), col(T.lt, NL - 1)).then_inc(sem.sC, 1)
    ve.wait_ge(sem.sC, 1)
    ve.wait_ge(sem.sO, 2)
    ve.tensor_scalar(T.ysb[0:Q, :], acc, col(T.r, 0), None, AluOpType.mult).then_inc(sem.sY, 1)

    ac.wait_ge(sem.sM, 1)
    for i in range(GE):
        ac.activation(ptcols(first[i], nb[i]), sbank(i), Exp, bias=col(T.negm, ME), scale=1.0,
                      accum_out=col(T.l, i)).then_inc(sem.sE, 1)
    ac.wait_ge(sem.sM, 2)
    ac.activation(col(T.w, 0), col(T.negm, ME), Exp, bias=col(T.negm, fin), scale=-1.0).then_inc(sem.sW, 1)
    for b in range(NL):
        ac.activation(ptcols(sl + b, 1), lcol(b), Exp, bias=col(T.negm, fin), scale=1.0,
                      accum_out=col(T.l, GE + b)).then_inc(sem.sEL, 1)

    g.sync.wait_ge(sem.sY, 1)
    g.sync.dma_start(T.y[:, :], T.ysb[0:Q, :]).then_inc(sem.st, 16)
    g.sync.wait_ge(sem.st, 16)
